import numpy as np
CORES = [19,147,275,403]
N = 4
S, B = 4, 64
def setup_inputs(rng):
    a = (rng.standard_normal((128, 128), dtype=np.float32) / 12)
    return {"x": rng.standard_normal((N, 128, S * B), dtype=np.float32), "a": np.broadcast_to(a, (N, 128, 128)).copy(), "at": np.broadcast_to(a.T, (N, 128, 128)).copy()}
def setup_inputs_big(rng):
    d = setup_inputs(rng)
    for k in ("x",): d[k] = (d[k].astype(np.float32) * 1048576.0).astype(d[k].dtype)
    return d
def setup_inputs_small(rng):
    d = setup_inputs(rng)
    for k in ("x",): d[k] = (d[k].astype(np.float32) * (1 / 1048576.0)).astype(d[k].dtype)
    return d
def setup_inputs_apart(rng):
    d = setup_inputs(rng)
    f = (10.0 ** rng.permutation(np.linspace(-1.5, 1.5, N))).astype(np.float32).reshape(N, 1, 1)
    for k in ("x",): d[k] = (d[k].astype(np.float32) * f).astype(d[k].dtype)
    return d
def reference(x, a, at):
    X, A = x.astype(np.float64), a.astype(np.float64)
    y = np.zeros((N, 128, S * B)); h = np.zeros((128, B))
    for r in range(N):
        for s in range(S):
            h = A[r].T @ h + X[r][:, B * s:B * s + B]
            y[r][:, B * s:B * s + B] = h
    return {"y": y.astype(np.float32)}

from concourse.mybir import AluOpType

S_, B_ = 4, 64
W_ = S_ * B_
KMAX = 8
P_ = 128

SCRATCH = {
    "xs": ("sbuf", [P_, W_], "float32"),
    "pw": ("sbuf", [P_, KMAX * P_], "float32"),
    "tw": ("sbuf", [P_, 2 * P_], "float32"),
    "land": ("sbuf", [P_, 3 * B_], "float32"),
    "ev": ("sbuf", [P_, B_], "float32"),
    "bs": ("sbuf", [P_, W_], "float32"),
    "ys": ("sbuf", [P_, W_], "float32"),
    "ph": ("psum", [P_, 512], "float32"),
    "p0": ("psum", [P_, 512], "float32"),
    "p1": ("psum", [P_, 512], "float32"),
    "pe": ("psum", [P_, 512], "float32"),
    "t0": ("psum", [P_, 512], "float32"),
    "t1": ("psum", [P_, 512], "float32"),
    "t2": ("psum", [P_, 512], "float32"),
    "t3": ("psum", [P_, 512], "float32"),
}
SEMAPHORES = (["la", "lx", "lat", "pmt", "pct", "e0m", "e0d", "em", "bd", "yd", "st", "sent"]
              + ["hm%d" % s for s in range(1, S_)] + ["hd%d" % s for s in range(1, S_)]
              + ["pm%d" % k for k in range(2, KMAX + 1)] + ["pc%d" % k for k in range(2, KMAX + 1)]
              + ["tm%d" % s for s in range(S_)] + ["arr%d" % q for q in range(3)])


def _routes(cores, topo):
    n = len(cores)
    way = {}
    for q in range(n):
        for r in range(q + 1, n):
            if topo.may_write(cores[q], cores[r]):
                way[(q, r)] = None
                continue
            mids = [m for m in range(n) if m != q and m != r
                    and topo.may_write(cores[q], cores[m]) and topo.may_write(cores[m], cores[r])]
            mids.sort(key=lambda m: 0 if q < m < r else 1)
            way[(q, r)] = mids[0]
    return way


def rank_program(g, core, T, topo):
    r = T.rank_of(core)
    if r is None:
        return
    cores = T.cores
    n = len(cores)
    sem = T.sem
    pe, dve, sy, sc = g.tensor, g.vector, g.sync, g.scalar
    queues = {"g": g, "pe": pe, "dve": dve, "sy": sy, "sc": sc}
    seen = set()

    def need(qn, name, val):
        if (qn, name, val) not in seen:
            seen.add((qn, name, val))
            queues[qn].wait_ge(sem[name], val)

    def blk(t, j, w=B_):
        return t[:, j * w:(j + 1) * w]

    def apow(k):
        return blk(T.pw, k - 1, P_)

    def engines(src, dst):
        return bin(topo.mask(cores[src], cores[dst])).count("1")

    way = _routes(cores, topo)
    passes = [(q, d) for (q, d), m in sorted(way.items()) if m == r]
    heads = sorted(set(m for (q, d), m in way.items() if q == r and m is not None))
    direct = [d for d in range(r + 1, n) if way[(r, d)] is None and d not in heads]
    srcs = list(range(r))
    late = [q for q in srcs if way[(q, r)] is not None]
    if not late and srcs:
        late = [srcs[-1]]
    assert len(late) <= 1
    early = [q for q in srcs if q not in late]
    from_of = {q: (q if way[(q, r)] is None else way[(q, r)]) for q in srcs}
    arrived = {q: engines(from_of[q], r) for q in srcs}
    for (q, d) in passes:
        if q not in arrived:
            arrived[q] = engines(q, r)
    dist = {q: r - 1 - q for q in srcs}
    top = max([S_ * (dist[q] + 1) for q in late] + [S_ * dist[q] for q in early] + ([S_] if early else []) + [1])

    sy.dma_start(apow(1), T.a[:]).then_inc(sem.la, 16)
    sc.dma_start(T.xs[:], T.x[:]).then_inc(sem.lx, 16)
    if top > 1:
        if heads:
            need("sy", "la", 16)
            need("sy", "lx", 16)
        sy.dma_start(blk(T.tw, 0, P_), T.at[:]).then_inc(sem.lat, 16)

    need("pe", "la", 16)
    need("pe", "lx", 16)
    need("dve", "lx", 16)
    for s in range(1, S_):
        if s > 1:
            need("pe", "hd%d" % (s - 1), 1)
        pe.matmul(T.ph[:, 0:B_], apow(1), blk(T.xs, s - 1), True, True).then_inc(sem["hm%d" % s], 1)
        need("dve", "hm%d" % s, 1)
        dve.tensor_tensor(blk(T.xs, s), T.ph[:, 0:B_], blk(T.xs, s), AluOpType.add).then_inc(sem["hd%d" % s], 1)

    sent = 0

    def send(src_ap, q, d):
        rid, pid = topo.addr(cores[d], core)
        g.remote_dma(blk(T.land, q), src_ap, sem["arr%d" % q], sem.sent, pid, rid, topo.mask(core, cores[d]))
        return engines(r, d)

    if heads or direct:
        need("g", "hd%d" % (S_ - 1), 1)
    for d in heads + direct:
        sent += send(blk(T.xs, S_ - 1), r, d)
    for (q, d) in passes:
        need("g", "arr%d" % q, arrived[q])
        sent += send(blk(T.land, q), q, d)
    if sent:
        need("g", "sent", sent)

    if not srcs:
        for s in range(1, S_):
            need("sy", "hd%d" % s, 1)
        sy.dma_start(T.y[:], T.xs[:]).then_inc(sem.st, 16)
        need("sy", "st", 16)
        return

    need("pe", "lat", 16)
    pe.matmul(T.p0[:, 0:P_], apow(1), blk(T.tw, 0, P_), True, True).then_inc(sem.pmt, 1)
    need("dve", "pmt", 1)
    dve.tensor_copy(blk(T.tw, 1, P_), T.p0[:, 0:P_]).then_inc(sem.pct, 1)
    pe.matmul(T.p1[:, 0:P_], blk(T.tw, 0, P_), apow(1), True, True).then_inc(sem.pm2, 1)
    need("dve", "pm2", 1)
    dve.tensor_copy(apow(2), T.p1[:, 0:P_]).then_inc(sem.pc2, 1)
    for k in range(3, top + 1):
        bank = T.p0 if k % 2 else T.p1
        need("pe", "pct", 1)
        if k > 3:
            need("pe", "pc%d" % (k - 2), 1)
        pe.matmul(bank[:, 0:P_], blk(T.tw, 1, P_), apow(k - 2), True, True).then_inc(sem["pm%d" % k], 1)
        need("dve", "pm%d" % k, 1)
        dve.tensor_copy(apow(k), bank[:, 0:P_]).then_inc(sem["pc%d" % k], 1)
    for k in range(2, top + 1):
        need("pe", "pc%d" % k, 1)

    for s in range(1, S_):
        need("dve", "hd%d" % s, 1)
    base = T.xs
    if early:
        far = [q for q in early if dist[q] > 0]
        near = [q for q in early if dist[q] == 0]
        e_ap = blk(T.land, near[0])
        if far:
            need("pe", "hd%d" % (S_ - 1), 1)
            for i, q in enumerate(far):
                need("pe", "arr%d" % q, arrived[q])
                pe.matmul(T.ph[:, 0:B_], apow(S_ * dist[q]), blk(T.land, q), i == 0, i == len(far) - 1
                          ).then_inc(sem.e0m, 1)
            need("dve", "e0m", len(far))
            need("dve", "arr%d" % near[0], arrived[near[0]])
            dve.tensor_tensor(T.ev[:], T.ph[:, 0:B_], e_ap, AluOpType.add).then_inc(sem.e0d, 1)
            need("pe", "e0d", 1)
            e_ap = T.ev[:]
        else:
            need("pe", "arr%d" % near[0], arrived[near[0]])
        for s in range(S_):
            pe.matmul(blk(T.pe, s), apow(s + 1), e_ap, True, True).then_inc(sem.em, 1)
        need("dve", "em", S_)
        dve.tensor_tensor(T.bs[:], T.pe[:, 0:W_], T.xs[:], AluOpType.add).then_inc(sem.bd, 1)
        need("dve", "bd", 1)
        base = T.bs

    q = late[0]
    need("pe", "arr%d" % q, arrived[q])
    for s in range(S_):
        bank = T["t%d" % s]
        pe.matmul(bank[:, 0:B_], apow(s + 1 + S_ * dist[q]), blk(T.land, q), True, True).then_inc(sem["tm%d" % s], 1)
        need("dve", "tm%d" % s, 1)
        dve.tensor_tensor(blk(T.ys, s), bank[:, 0:B_], blk(base, s), AluOpType.add).then_inc(sem.yd, 1)
    need("sy", "yd", S_)
    sy.dma_start(T.y[:], T.ys[:]).then_inc(sem.st, 16)
    need("sy", "st", 16)
